import numpy as np
import ml_dtypes


def mxq(x, axis, fmt="e4m3"):
    dtype, down = {"e4m3": (ml_dtypes.float8_e4m3fn, 7), "e5m2": (ml_dtypes.float8_e5m2, 14)}[fmt]
    v = np.moveaxis(np.asarray(x, np.float32).astype(ml_dtypes.bfloat16).astype(np.float64), axis, -1)
    blocks = v.reshape(v.shape[:-1] + (-1, 32))
    amax = np.abs(blocks).max(-1, keepdims=True)
    byte = np.maximum(np.where(amax > 0, np.frexp(amax)[1] - 1 + 127, 0) - down, 1)
    scale = np.exp2(byte - 127.0)
    codes = (blocks / scale).astype(np.float32).astype(dtype).astype(np.float64)
    return np.moveaxis((codes * scale).reshape(v.shape), -1, axis)


WIDE = False


def mx_kscale(k):
    if not WIDE:
        return np.ones(k)
    levels = np.array([10, -10, 5, -5, 0])
    if k % 512:
        return np.exp2(np.random.permutation(np.resize(levels, k // 32))).repeat(32)
    a = np.empty((k // 512, 16))
    for p in range(k // 512):
        a[p, :8] = np.random.permutation(np.resize(levels, 8))
        for g in range(8):
            far = levels[np.abs(levels - a[p, g]) >= 10]
            a[p, g + 8] = far[np.random.randint(len(far))]
    return np.exp2(a.ravel()).repeat(32)


def f64(x):
    return np.asarray(x).astype(np.float64)


def striped(idx):
    return np.tile(idx.reshape(-1, 16).T, (8, 1)).astype(np.uint16)


def unstriped(offs):
    return offs[:16].T.reshape(-1).astype(np.int64)


def pack_weight(w):
    k, n = w.shape
    w = f64(np.asarray(w, np.float32).astype(ml_dtypes.bfloat16)).reshape(k // 32, 32, n)
    amax = np.abs(w).max(1)
    byte = np.clip(np.where(amax > 0, np.frexp(amax)[1] - 1 + 127 - 7, 1), 1, 254)
    scaled = (w * np.exp2(127.0 - byte)[:, None, :]).reshape(k, n).astype(np.float32)
    words = np.ascontiguousarray(scaled.reshape(k // 512, 128, 4, n).transpose(0, 1, 3, 2)).astype(ml_dtypes.float8_e4m3fn).view(np.uint8)
    return words, np.ascontiguousarray(byte.astype(np.uint8).reshape(k // 512, 16, n))


def unpack_weight(words, scales):
    g, p, n, _ = words.shape
    vals = np.ascontiguousarray(words).view(ml_dtypes.float8_e4m3fn).astype(np.float64) * np.repeat(np.exp2(scales.astype(np.float64) - 127.0), 8, axis=1)[..., None]
    return vals.transpose(0, 1, 3, 2).reshape(g * 512, n)


E2M1 = np.array([0.0, 0.5, 1.0, 1.5, 2.0, 3.0, 4.0, 6.0, -0.0, -0.5, -1.0, -1.5, -2.0, -3.0, -4.0, -6.0])


def pack_fp4(w):
    k, n = w.shape
    w = f64(np.asarray(w, np.float32).astype(ml_dtypes.bfloat16)).reshape(k // 32, 32, n)
    amax = np.abs(w).max(1)
    mant, ex = np.frexp(amax / 6.0)
    byte = np.clip(np.where(amax > 0, np.where(mant > 0.5, ex, ex - 1) + 127, 1), 1, 254)
    scaled = (w * np.exp2(127.0 - byte)[:, None, :]).reshape(k, n).astype(np.float32)
    c = np.ascontiguousarray(scaled.reshape(k // 512, 128, 4, n).transpose(0, 1, 3, 2)).astype(ml_dtypes.float4_e2m1fn).view(np.uint8) & 0xF
    words = (c[..., 0::2] | (c[..., 1::2] << 4)).reshape(k // 512, 128, 2 * n)
    return np.ascontiguousarray(words), np.ascontiguousarray(byte.astype(np.uint8).reshape(k // 512, 16, n))


def unpack_fp4(words, scales):
    g, _, n = scales.shape
    words = np.ascontiguousarray(words).reshape(g, 128, n, 2)
    nib = np.empty((g, 128, n, 4), np.uint8)
    nib[..., 0::2] = words & 0xF
    nib[..., 1::2] = words >> 4
    vals = E2M1[nib] * np.repeat(np.exp2(scales.astype(np.float64) - 127.0), 8, axis=1)[..., None]
    return vals.transpose(0, 1, 3, 2).reshape(g * 512, n)


def sigmoid(v):
    return 1.0 / (1.0 + np.exp(-np.maximum(v, -700.0)))


K, T, S, D, N, H, V, U = 512, 4096, 1024, 4, 128, 512, 256, 512


def setup_inputs():
    n = np.random.standard_normal
    s = mx_kscale(K)[:, None]
    u = mx_kscale(H)
    packed_xT = pack_weight(n((K, T)) * s)
    packed_w1 = pack_fp4(n((K, H)) / np.sqrt(K) / s)
    packed_w2 = pack_fp4(n((K, H)) / np.sqrt(K) / s)
    packed_w3 = pack_fp4(n((H, N)) / np.sqrt(H) / u[:, None])
    return {
        "x_words": packed_xT[0],
        "x_scales": packed_xT[1],
        "w1_words": packed_w1[0],
        "w1_scales": packed_w1[1],
        "w2_words": packed_w2[0],
        "w2_scales": packed_w2[1],
        "mask": (np.random.uniform(0.2, 1.0, (H, S))).astype(np.float32),
        "unit": (np.random.uniform(0.6, 1.4, (H, 1)) * u[:, None]).astype(np.float32),
        "w3_words": packed_w3[0],
        "w3_scales": packed_w3[1],
        "offs": striped(np.random.permutation(T)[:S]),
        "exp_": striped(np.random.permutation(S)),
        "per": striped(np.random.permutation(np.concatenate([np.arange(V), np.random.randint(0, V, U - V)]))),
    }


def reference(x_words, x_scales, w1_words, w1_scales, w2_words, w2_scales, mask, unit, w3_words, w3_scales, offs, exp_, per):
    xq = unpack_weight(x_words, x_scales)[:, unstriped(offs)]
    inf = unpack_fp4(w1_words, w1_scales).T @ xq
    load = np.log(np.exp(inf) + 1.0)
    ie = load[:, unstriped(exp_)]
    dose = ie * f64(mask)
    sus = unpack_fp4(w2_words, w2_scales).T @ xq
    susc = sigmoid(sus)
    haz = (dose / (dose + 1.0)) * susc
    toth = haz.reshape(len(haz), -1, D).sum(axis=2)
    pinf = -1.0 * np.exp(-1.0 * toth) + 1.0
    pp = pinf[:, unstriped(per)]
    mxd = dose.reshape(len(dose), -1, D).max(axis=2)
    md = mxd[:, unstriped(per)]
    hid = f64(unit) * (pp * md)
    return unpack_fp4(w3_words, w3_scales).T @ mxq(hid, 0, "e4m3")

@@ -1,0 +1,251 @@
+from contextlib import ExitStack
+
+import concourse.mybir as mybir
+from concourse.masks import make_identity
+
+K, T, S, D, N, H, V, U = 512, 4096, 1024, 4, 128, 512, 256, 512
+FLOPS = 2 * K * H * S * 2 + 2 * H * N * U
+
+F32 = mybir.dt.float32
+BF16 = mybir.dt.bfloat16
+I32 = mybir.dt.int32
+U32 = mybir.dt.uint32
+U16 = mybir.dt.uint16
+U8 = mybir.dt.uint8
+FP8X4 = mybir.dt.float8_e4m3fn_x4
+FP4X4 = mybir.dt.float4_e2m1fn_x4
+ACT = mybir.ActivationFunctionType
+ALU = mybir.AluOpType
+
+P = 128
+PACK = 4
+BANK = 512
+HALVES = S // BANK
+LN_FLOOR = 2.0**-63
+
+
+def load_scale_rows(queues, plane, rows):
+    for q, queue in enumerate(queues):
+        queue.dma_start(out=plane[32 * q : 32 * q + 4, :].bitcast(I32), in_=rows[4 * q : 4 * q + 4, :].bitcast(I32))
+
+
+def deal_words(nc, dealt, raw):
+    nc.vector.tensor_copy(
+        out=dealt[:].rearrange("p (t m b) -> p t m b", t=PACK, b=2),
+        in_=raw[:].rearrange("p (m t b) -> p t m b", t=PACK, b=2),
+    )
+
+
+def deal_scales(nc, dealt, raw):
+    nc.vector.tensor_copy(
+        out=dealt[:].rearrange("p (t m) -> p t m", t=PACK),
+        in_=raw[:].rearrange("p (m t) -> p t m", t=PACK),
+    )
+
+
+def tile_picked_yepitpr_dose_p_kernel(
+    tc, x_words, x_scales, w1_words, w1_scales, w2_words, w2_scales, mask, unit, w3_words, w3_scales, offs, exp_, per, out
+):
+    nc = tc.nc
+    with ExitStack() as ctx:
+        keep = ctx.enter_context(tc.tile_pool(name="keep", bufs=1))
+        psum = ctx.enter_context(tc.psum_pool(name="psum", bufs=1))
+
+        def sb(name, shape, dtype):
+            return keep.tile(shape, dtype, name=name, align_bytes=64)
+
+        def bank(b, width=BANK):
+            return psum.tile([P, width], F32, name="bank%d" % b)
+
+        offs_t = sb("offs_t", [P, S // 16], U16)
+        exp_t = sb("exp_t", [P, S // 16], U16)
+        per_t = sb("per_t", [P, U // 16], U16)
+        xw_all = sb("xw_all", [P, T], I32)
+        xs_all = sb("xs_all", [P, T], U8)
+        w_raw = sb("w_raw", [P, 2 * H], U8)
+        ws_raw = sb("ws_raw", [P, H], U8)
+        ident = sb("ident", [P, P], F32)
+        w3w = sb("w3w", [P, 2 * N], U8)
+        w3s = sb("w3s", [P, N], U8)
+        unit_t = sb("unit_t", [P, PACK], F32)
+
+        nc.vector.memset(xs_all[:].bitcast(I32), 0)
+        nc.gpsimd.memset(ws_raw[:].bitcast(I32), 0)
+
+        nc.sync.dma_start(offs_t[:], offs)
+        nc.scalar.dma_start(out=w_raw[:].bitcast(I32), in_=w1_words[0].bitcast(I32))
+        nc.sync.dma_start(exp_t[:], exp_)
+        nc.sync.dma_start(per_t[:], per)
+        nc.sync.dma_start(out=xw_all[:], in_=x_words[0].rearrange("p c r -> p (c r)").bitcast(I32))
+        load_scale_rows([nc.scalar] * 3 + [nc.gpsimd], ws_raw, w1_scales[0])
+        load_scale_rows([nc.scalar] * 4, xs_all, x_scales[0])
+
+        w1w = sb("w1w", [P, 2 * H], U8)
+        w1s = sb("w1s", [P, H], U8)
+        w2w = sb("w2w", [P, 2 * H], U8)
+        w2s = sb("w2s", [P, H], U8)
+        xs = [sb("xs%d" % h, [P, BANK], U8) for h in range(HALVES)]
+        xw = [sb("xw%d" % h, [P, BANK], U32) for h in range(HALVES)]
+        cols = BANK // 16
+        deal_words(nc, w1w, w_raw)
+        deal_scales(nc, w1s, ws_raw)
+        for h in range(HALVES):
+            picked = offs_t[:, h * cols : (h + 1) * cols]
+            nc.vector.tensor_copy(xs[h][:], xs_all[:].indirect(picked))
+            nc.vector.tensor_copy(xw[h][:], xw_all[:].bitcast(U32).indirect(picked))
+
+        nc.sync.dma_start(out=w_raw[:].bitcast(I32), in_=w2_words[0].bitcast(I32))
+        load_scale_rows([nc.sync] * 4, ws_raw, w2_scales[0])
+        mask_rows = mask.rearrange("(p t) s -> p t s", t=PACK)
+        mask_first = sb("xs_all", [P, S], F32)
+        mask_rest = sb("xw_all", [P, PACK - 1, S], F32)
+        nc.sync.dma_start(out=mask_first[:], in_=mask_rows[:, 0, :])
+        nc.sync.dma_start(out=mask_rest[:], in_=mask_rows[:, 1:PACK, :])
+        mask_t = [mask_first[:]] + [mask_rest[:, t, :] for t in range(PACK - 1)]
+
+        nc.gpsimd.memset(w3s[:].bitcast(I32), 0)
+        make_identity(nc, ident[:])
+        nc.gpsimd.dma_start(out=unit_t[:], in_=unit.rearrange("(p t) o -> p (t o)", t=PACK))
+        nc.gpsimd.dma_start(out=w3w[:].bitcast(I32), in_=w3_words[0].bitcast(I32))
+        load_scale_rows([nc.gpsimd] * 4, w3s, w3_scales[0])
+
+        def product(words, scales, t, h):
+            acc = bank(HALVES * t + h)
+            nc.tensor.matmul_mx(
+                out=acc[:],
+                lhsT=words[:, 2 * P * t : 2 * P * (t + 1)].bitcast(FP4X4),
+                lhsT_scale=scales[:, P * t : P * (t + 1)],
+                rhs=xw[h][:].bitcast(FP8X4),
+                rhs_scale=xs[h][:],
+                start=True,
+                stop=True,
+            )
+            return acc
+
+        def half(tile, h):
+            return tile[:, BANK * h : BANK * (h + 1)]
+
+        inf = {}
+        sneg = [sb("sneg%d" % t, [P, S], F32) for t in range(PACK)]
+        for h in range(HALVES):
+            for t in range(PACK):
+                inf[t, h] = product(w1w, w1s, t, h)
+                nc.scalar.activation(half(sneg[t], h), inf[t, h][:], ACT.Sigmoid, scale=-1.0)
+
+        deal_words(nc, w2w, w_raw)
+        deal_scales(nc, w2s, ws_raw)
+        neg_unit = sb("neg_unit", [P, PACK], F32)
+        nc.vector.tensor_scalar(neg_unit[:], unit_t[:], -1.0, None, ALU.mult)
+
+        lsig = [sb("lsig%d" % t, [P, S], F32) for t in range(PACK)]
+        load = [sb("load%d" % t, [P, S], F32) for t in range(PACK)]
+        dose = [sb("dose%d" % t, [P, S], F32) for t in range(PACK)]
+        susc = [sb("susc%d" % t, [P, S], F32) for t in range(PACK)]
+        for t in range(PACK):
+            nc.scalar.activation(lsig[t][:], sneg[t][:], ACT.Ln, bias=LN_FLOOR)
+
+        def make_load(t):
+            for h in range(HALVES):
+                nc.vector.scalar_tensor_tensor(half(load[t], h), half(lsig[t], h), -1.0, inf[t, h][:], ALU.mult, ALU.max)
+
+        def make_dose(t):
+            for h in range(HALVES):
+                nc.vector.tensor_tensor(
+                    half(dose[t], h), load[t][:].indirect(exp_t[:, h * cols : (h + 1) * cols]), half(mask_t[t], h), ALU.mult
+                )
+
+        make_load(0)
+        make_load(1)
+        make_dose(0)
+        make_load(2)
+        make_load(3)
+        for t in range(PACK):
+            for h in range(HALVES):
+                sus = product(w2w, w2s, t, h)
+                nc.scalar.activation(
+                    half(susc[t], h).rearrange("p (d v) -> p d v", d=D), sus[:].rearrange("p (v d) -> p d v", d=D), ACT.Sigmoid
+                )
+        for t in range(1, PACK):
+            make_dose(t)
+
+        ln1p = [sb("lsig%d" % t, [P, S], F32) for t in range(PACK)]
+        for t in range(PACK):
+            nc.scalar.activation(ln1p[t][:], dose[t][:], ACT.Ln, bias=1.0)
+
+        def fold(out_ap, pairs_ap, src, op):
+            quads = src[:].rearrange("p (v d) -> p v d", d=D)
+            pairs = pairs_ap.rearrange("p (v d) -> p v d", d=2)
+            nc.vector.tensor_tensor(pairs, quads[:, :, 0:2], quads[:, :, 2:4], op)
+            nc.vector.tensor_tensor(out_ap, pairs[:, :, 0], pairs[:, :, 1], op)
+
+        group = [sb("group%d" % t, [P, 3 * V], F32) for t in range(PACK)]
+        weight = [sb("weight%d" % t, [P, V], F32) for t in range(PACK)]
+        for t in range(PACK):
+            mxd = sb("mxd%d" % t, [P, V], F32)
+            fold(mxd[:], group[t][:, V : 3 * V], dose[t], ALU.max)
+            nc.vector.tensor_scalar(weight[t][:], mxd[:], neg_unit[:, t : t + 1], None, ALU.mult)
+
+        recip = [sb("sneg%d" % t, [P, S], F32) for t in range(PACK)]
+        for t in range(PACK):
+            nc.scalar.activation(
+                recip[t][:].rearrange("p (h d v) -> p h v d", h=HALVES, d=D),
+                ln1p[t][:].rearrange("p (h v d) -> p h v d", h=HALVES, d=D),
+                ACT.Exp,
+                scale=-1.0,
+            )
+        neg_haz = [sb("load%d" % t, [P, HALVES, D, P], F32) for t in range(PACK)]
+        for t in range(PACK):
+            nc.vector.scalar_tensor_tensor(
+                neg_haz[t][:].rearrange("p h d v -> p (h d v)"), recip[t][:], 1.0, susc[t][:], ALU.subtract, ALU.mult
+            )
+
+        def escape_by_transposes(t):
+            turned = bank(HALVES * t, V)
+            for h in range(HALVES):
+                for d in range(D):
+                    nc.tensor.matmul(
+                        turned[:, P * h : P * (h + 1)], neg_haz[t][:, h, d, :], ident[:], start=(d == 0), stop=(d == D - 1), is_transpose=True
+                    )
+            escape_turned = sb("escape%d" % t, [P, V], F32)
+            nc.scalar.activation(escape_turned[:], turned[:], ACT.Exp)
+            escape = bank(HALVES * t + 1, V)
+            for h in range(HALVES):
+                nc.tensor.transpose(escape[:, P * h : P * (h + 1)], escape_turned[:, P * h : P * (h + 1)], ident[:])
+            return escape
+
+        def escape_by_vector(t):
+            pair_sum = sb("pair_sum", [P, HALVES, 2, P], F32)
+            neg_toth = sb("neg_toth", [P, HALVES, P], F32)
+            nc.vector.tensor_tensor(pair_sum[:], neg_haz[t][:, :, 0:2, :], neg_haz[t][:, :, 2:4, :], ALU.add)
+            nc.vector.tensor_tensor(neg_toth[:], pair_sum[:, :, 0, :], pair_sum[:, :, 1, :], ALU.add)
+            escape = sb("escape%d" % t, [P, V], F32)
+            nc.scalar.activation(escape[:], neg_toth[:].rearrange("p h v -> p (h v)"), ACT.Exp)
+            return escape
+
+        UH = U // 2
+        planes = [sb("planes%d" % j, [P, PACK, UH], BF16) for j in range(2)]
+        escapes = [escape_by_transposes(t) for t in range(PACK - 1)] + [escape_by_vector(PACK - 1)]
+        for t in range(PACK):
+            nc.vector.scalar_tensor_tensor(group[t][:, 0:V], escapes[t][:], 1.0, weight[t][:], ALU.subtract, ALU.mult)
+            for j in range(2):
+                people = group[t][:].indirect(per_t[:, j * UH // 16 : (j + 1) * UH // 16])
+                if t == PACK - 1 and j == 0:
+                    nc.vector.tensor_copy(planes[j][:, t, :], people)
+                else:
+                    nc.scalar.activation(planes[j][:, t, :], people, ACT.Copy)
+
+        for j in range(2):
+            r = slice(j * UH, (j + 1) * UH)
+            hid = sb("hid%d" % j, [P, UH, PACK], BF16)
+            hq = sb("hq%d" % j, [P, UH], U32)
+            hs = sb("hs%d" % j, [P, UH], U8)
+            res = sb("res%d" % j, [P, UH], F32)
+            nc.vector.tensor_copy(hid[:], planes[j][:].rearrange("p t r -> p r t"))
+            nc.vector.quantize_mx(out=hq[:].bitcast(FP8X4), scales=hs[:], in_=hid[:].rearrange("p r t -> p (r t)"))
+            acc = bank(HALVES * (PACK - 1) + j, UH)
+            nc.tensor.matmul_mx(
+                out=acc[:], lhsT=w3w[:].bitcast(FP4X4), lhsT_scale=w3s[:], rhs=hq[:].bitcast(FP8X4), rhs_scale=hs[:],
+                start=True, stop=True,
+            )
+            nc.scalar.copy(res[:], acc[:])
+            nc.sync.dma_start(out=out[:, r], in_=res[:])

@@ -26,7 +26,7 @@ LN_FLOOR = 2.0**-63
 
 def load_scale_rows(queues, plane, rows):
     for q, queue in enumerate(queues):
-        queue.dma_start(out=plane[32 * q : 32 * q + 4, :].bitcast(I32), in_=rows[4 * q : 4 * q + 4, :].bitcast(I32))
+        queue.dma_start(out=plane[32 * q : 32 * q + 4].bitcast(I32), in_=rows[4 * q : 4 * q + 4, :].bitcast(I32))
 
 
 def deal_words(nc, dealt, raw):
@@ -65,20 +65,18 @@ def tile_picked_yepitpr_dose_p_kernel(
         w_raw = sb("w_raw", [P, 2 * H], U8)
         ws_raw = sb("ws_raw", [P, H], U8)
         ident = sb("ident", [P, P], F32)
-        w3w = sb("w3w", [P, 2 * N], U8)
-        w3s = sb("w3s", [P, N], U8)
         unit_t = sb("unit_t", [P, PACK], F32)
 
         nc.vector.memset(xs_all[:].bitcast(I32), 0)
-        nc.gpsimd.memset(ws_raw[:].bitcast(I32), 0)
+        nc.vector.memset(ws_raw[:].bitcast(I32), 0)
 
         nc.sync.dma_start(offs_t[:], offs)
-        nc.scalar.dma_start(out=w_raw[:].bitcast(I32), in_=w1_words[0].bitcast(I32))
+        nc.sync.dma_start(out=w_raw[:].bitcast(I32), in_=w1_words[0].bitcast(I32))
         nc.sync.dma_start(exp_t[:], exp_)
         nc.sync.dma_start(per_t[:], per)
         nc.sync.dma_start(out=xw_all[:], in_=x_words[0].rearrange("p c r -> p (c r)").bitcast(I32))
-        load_scale_rows([nc.scalar] * 3 + [nc.gpsimd], ws_raw, w1_scales[0])
-        load_scale_rows([nc.scalar] * 4, xs_all, x_scales[0])
+        load_scale_rows([nc.gpsimd] + [nc.scalar] * 3, xs_all, x_scales[0])
+        load_scale_rows([nc.scalar] * 4, ws_raw, w1_scales[0])
 
         w1w = sb("w1w", [P, 2 * H], U8)
         w1s = sb("w1s", [P, H], U8)
@@ -94,7 +92,7 @@ def tile_picked_yepitpr_dose_p_kernel(
             nc.vector.tensor_copy(xs[h][:], xs_all[:].indirect(picked))
             nc.vector.tensor_copy(xw[h][:], xw_all[:].bitcast(U32).indirect(picked))
 
-        nc.sync.dma_start(out=w_raw[:].bitcast(I32), in_=w2_words[0].bitcast(I32))
+        nc.gpsimd.dma_start(out=w_raw[:].bitcast(I32), in_=w2_words[0].bitcast(I32))
         load_scale_rows([nc.sync] * 4, ws_raw, w2_scales[0])
         mask_rows = mask.rearrange("(p t) s -> p t s", t=PACK)
         mask_first = sb("xs_all", [P, S], F32)
@@ -103,11 +101,10 @@ def tile_picked_yepitpr_dose_p_kernel(
         nc.sync.dma_start(out=mask_rest[:], in_=mask_rows[:, 1:PACK, :])
         mask_t = [mask_first[:]] + [mask_rest[:, t, :] for t in range(PACK - 1)]
 
-        nc.gpsimd.memset(w3s[:].bitcast(I32), 0)
         make_identity(nc, ident[:])
+        minus_one = sb("minus_one", [P, P], F32)
+        nc.gpsimd.memset(minus_one[:], -1.0)
         nc.gpsimd.dma_start(out=unit_t[:], in_=unit.rearrange("(p t) o -> p (t o)", t=PACK))
-        nc.gpsimd.dma_start(out=w3w[:].bitcast(I32), in_=w3_words[0].bitcast(I32))
-        load_scale_rows([nc.gpsimd] * 4, w3s, w3_scales[0])
 
         def product(words, scales, t, h):
             acc = bank(HALVES * t + h)
@@ -134,6 +131,10 @@ def tile_picked_yepitpr_dose_p_kernel(
 
         deal_words(nc, w2w, w_raw)
         deal_scales(nc, w2s, ws_raw)
+        w3w = w_raw[:, 0 : 2 * N]
+        w3s = ws_raw[:, 0:N]
+        nc.sync.dma_start(out=w3w.bitcast(I32), in_=w3_words[0].bitcast(I32))
+        load_scale_rows([nc.sync] * 4, w3s, w3_scales[0])
         neg_unit = sb("neg_unit", [P, PACK], F32)
         nc.vector.tensor_scalar(neg_unit[:], unit_t[:], -1.0, None, ALU.mult)
 
@@ -141,7 +142,9 @@ def tile_picked_yepitpr_dose_p_kernel(
         load = [sb("load%d" % t, [P, S], F32) for t in range(PACK)]
         dose = [sb("dose%d" % t, [P, S], F32) for t in range(PACK)]
         susc = [sb("susc%d" % t, [P, S], F32) for t in range(PACK)]
-        for t in range(PACK):
+        for h in range(HALVES):
+            nc.scalar.activation(half(lsig[0], h), half(sneg[0], h), ACT.Ln, bias=LN_FLOOR)
+        for t in range(1, PACK):
             nc.scalar.activation(lsig[t][:], sneg[t][:], ACT.Ln, bias=LN_FLOOR)
 
         def make_load(t):
@@ -172,34 +175,35 @@ def tile_picked_yepitpr_dose_p_kernel(
         for t in range(PACK):
             nc.scalar.activation(ln1p[t][:], dose[t][:], ACT.Ln, bias=1.0)
 
-        def fold(out_ap, pairs_ap, src, op):
-            quads = src[:].rearrange("p (v d) -> p v d", d=D)
-            pairs = pairs_ap.rearrange("p (v d) -> p v d", d=2)
-            nc.vector.tensor_tensor(pairs, quads[:, :, 0:2], quads[:, :, 2:4], op)
-            nc.vector.tensor_tensor(out_ap, pairs[:, :, 0], pairs[:, :, 1], op)
-
         group = [sb("group%d" % t, [P, 3 * V], F32) for t in range(PACK)]
-        weight = [sb("weight%d" % t, [P, V], F32) for t in range(PACK)]
-        for t in range(PACK):
-            mxd = sb("mxd%d" % t, [P, V], F32)
-            fold(mxd[:], group[t][:, V : 3 * V], dose[t], ALU.max)
-            nc.vector.tensor_scalar(weight[t][:], mxd[:], neg_unit[:, t : t + 1], None, ALU.mult)
+        mxd = [sb("mxd%d" % t, [P, V], F32) for t in range(PACK)]
+        for pair in ((0, 1), (2, 3)):
+            for t in pair:
+                quads = dose[t][:].rearrange("p (v d) -> p v d", d=D)
+                nc.vector.tensor_tensor(
+                    group[t][:, V : 3 * V].rearrange("p (v d) -> p v d", d=2), quads[:, :, 0:2], quads[:, :, 2:4], ALU.max
+                )
+            for t in pair:
+                pairs = group[t][:, V : 3 * V].rearrange("p (v d) -> p v d", d=2)
+                nc.vector.tensor_tensor(mxd[t][:], pairs[:, :, 0], pairs[:, :, 1], ALU.max)
 
         recip = [sb("sneg%d" % t, [P, S], F32) for t in range(PACK)]
-        for t in range(PACK):
+        neg_haz = [sb("load%d" % t, [P, HALVES, D, P], F32) for t in range(PACK)]
+
+        last = PACK - 1
+        weight = sb("weight", [P, V], F32)
+        nc.vector.tensor_scalar(weight[:], mxd[last][:], neg_unit[:, last : last + 1], None, ALU.mult)
+
+        for t in range(PACK - 1):
             nc.scalar.activation(
                 recip[t][:].rearrange("p (h d v) -> p h v d", h=HALVES, d=D),
                 ln1p[t][:].rearrange("p (h v d) -> p h v d", h=HALVES, d=D),
                 ACT.Exp,
                 scale=-1.0,
             )
-        neg_haz = [sb("load%d" % t, [P, HALVES, D, P], F32) for t in range(PACK)]
-        for t in range(PACK):
             nc.vector.scalar_tensor_tensor(
                 neg_haz[t][:].rearrange("p h d v -> p (h d v)"), recip[t][:], 1.0, susc[t][:], ALU.subtract, ALU.mult
             )
-
-        def escape_by_transposes(t):
             turned = bank(HALVES * t, V)
             for h in range(HALVES):
                 for d in range(D):
@@ -210,42 +214,53 @@ def tile_picked_yepitpr_dose_p_kernel(
             nc.scalar.activation(escape_turned[:], turned[:], ACT.Exp)
             escape = bank(HALVES * t + 1, V)
             for h in range(HALVES):
-                nc.tensor.transpose(escape[:, P * h : P * (h + 1)], escape_turned[:, P * h : P * (h + 1)], ident[:])
-            return escape
+                cols_h = slice(P * h, P * (h + 1))
+                nc.tensor.matmul(escape[:, cols_h], minus_one[:], ident[:], start=True, stop=False, is_transpose=True)
+                nc.tensor.matmul(escape[:, cols_h], escape_turned[:, cols_h], ident[:], start=False, stop=True, is_transpose=True)
+            nc.vector.scalar_tensor_tensor(group[t][:, 0:V], mxd[t][:], neg_unit[:, t : t + 1], escape[:], ALU.mult, ALU.mult)
 
-        def escape_by_vector(t):
-            pair_sum = sb("pair_sum", [P, HALVES, 2, P], F32)
-            neg_toth = sb("neg_toth", [P, HALVES, P], F32)
-            nc.vector.tensor_tensor(pair_sum[:], neg_haz[t][:, :, 0:2, :], neg_haz[t][:, :, 2:4, :], ALU.add)
-            nc.vector.tensor_tensor(neg_toth[:], pair_sum[:, :, 0, :], pair_sum[:, :, 1, :], ALU.add)
-            escape = sb("escape%d" % t, [P, V], F32)
-            nc.scalar.activation(escape[:], neg_toth[:].rearrange("p h v -> p (h v)"), ACT.Exp)
-            return escape
+        t = PACK - 1
+        pair_sum = sb("pair_sum", [P, HALVES, 2, P], F32)
+        neg_toth = sb("neg_toth", [P, HALVES, P], F32)
+        for h in range(HALVES):
+            nc.scalar.activation(
+                half(recip[t], h).rearrange("p (d v) -> p v d", d=D), half(ln1p[t], h).rearrange("p (v d) -> p v d", d=D), ACT.Exp, scale=-1.0
+            )
+            nc.vector.scalar_tensor_tensor(
+                neg_haz[t][:, h].rearrange("p d v -> p (d v)"), half(recip[t], h), 1.0, half(susc[t], h), ALU.subtract, ALU.mult
+            )
+        for h in range(HALVES):
+            nc.vector.tensor_tensor(pair_sum[:, h], neg_haz[t][:, h, 0:2, :], neg_haz[t][:, h, 2:4, :], ALU.add)
+        nc.vector.tensor_tensor(neg_toth[:], pair_sum[:, :, 0, :], pair_sum[:, :, 1, :], ALU.add)
+        escape = sb("escape%d" % t, [P, V], F32)
+        nc.scalar.activation(escape[:], neg_toth[:].rearrange("p h v -> p (h v)"), ACT.Exp)
+        nc.vector.scalar_tensor_tensor(group[t][:, 0:V], escape[:], 1.0, weight[:], ALU.subtract, ALU.mult)
 
         UH = U // 2
         planes = [sb("planes%d" % j, [P, PACK, UH], BF16) for j in range(2)]
-        escapes = [escape_by_transposes(t) for t in range(PACK - 1)] + [escape_by_vector(PACK - 1)]
         for t in range(PACK):
-            nc.vector.scalar_tensor_tensor(group[t][:, 0:V], escapes[t][:], 1.0, weight[t][:], ALU.subtract, ALU.mult)
             for j in range(2):
                 people = group[t][:].indirect(per_t[:, j * UH // 16 : (j + 1) * UH // 16])
-                if t == PACK - 1 and j == 0:
+                if t >= 2 and j == 0:
                     nc.vector.tensor_copy(planes[j][:, t, :], people)
                 else:
                     nc.scalar.activation(planes[j][:, t, :], people, ACT.Copy)
 
+        hid = [sb("hid%d" % j, [P, UH, PACK], BF16) for j in range(2)]
+        hq = [sb("hq%d" % j, [P, UH], U32) for j in range(2)]
+        hs = [sb("hs%d" % j, [P, UH], U8) for j in range(2)]
         for j in range(2):
-            r = slice(j * UH, (j + 1) * UH)
-            hid = sb("hid%d" % j, [P, UH, PACK], BF16)
-            hq = sb("hq%d" % j, [P, UH], U32)
-            hs = sb("hs%d" % j, [P, UH], U8)
-            res = sb("res%d" % j, [P, UH], F32)
-            nc.vector.tensor_copy(hid[:], planes[j][:].rearrange("p t r -> p r t"))
-            nc.vector.quantize_mx(out=hq[:].bitcast(FP8X4), scales=hs[:], in_=hid[:].rearrange("p r t -> p (r t)"))
+            nc.vector.tensor_copy(
+                hid[j][:].rearrange("p (c i) t -> p c t i", i=4), planes[j][:].rearrange("p t (c i) -> p c t i", i=4)
+            )
+        for j in range(2):
+            nc.vector.quantize_mx(out=hq[j][:].bitcast(FP8X4), scales=hs[j][:], in_=hid[j][:].rearrange("p r t -> p (r t)"))
+        for j, queue in enumerate((nc.sync, nc.scalar)):
             acc = bank(HALVES * (PACK - 1) + j, UH)
             nc.tensor.matmul_mx(
-                out=acc[:], lhsT=w3w[:].bitcast(FP4X4), lhsT_scale=w3s[:], rhs=hq[:].bitcast(FP8X4), rhs_scale=hs[:],
+                out=acc[:], lhsT=w3w.bitcast(FP4X4), lhsT_scale=w3s, rhs=hq[j][:].bitcast(FP8X4), rhs_scale=hs[j][:],
                 start=True, stop=True,
             )
+            res = sb("res%d" % j, [P, UH], F32)
             nc.scalar.copy(res[:], acc[:])
-            nc.sync.dma_start(out=out[:, r], in_=res[:])
+            queue.dma_start(out=out[:, j * UH : (j + 1) * UH], in_=res[:])

@@ -49,6 +49,7 @@ def tile_picked_yepitpr_dose_p_kernel(
     nc = tc.nc
     with ExitStack() as ctx:
         keep = ctx.enter_context(tc.tile_pool(name="keep", bufs=1))
+        reused = ctx.enter_context(tc.tile_pool(name="reused", bufs=1))
         psum = ctx.enter_context(tc.psum_pool(name="psum", bufs=1))
 
         def sb(name, shape, dtype):
@@ -60,28 +61,28 @@ def tile_picked_yepitpr_dose_p_kernel(
         offs_t = sb("offs_t", [P, S // 16], U16)
         exp_t = sb("exp_t", [P, S // 16], U16)
         per_t = sb("per_t", [P, U // 16], U16)
-        xw_all = sb("xw_all", [P, T], I32)
+        xw_all = reused.tile([P, T], I32, name="xw_all", align_bytes=64, offset=0)
         xs_all = sb("xs_all", [P, T], U8)
         w_raw = sb("w_raw", [P, 2 * H], U8)
         ws_raw = sb("ws_raw", [P, H], U8)
         ident = sb("ident", [P, P], F32)
         unit_t = sb("unit_t", [P, PACK], F32)
 
+        nc.gpsimd.memset(ws_raw[:].bitcast(I32), 0)
         nc.vector.memset(xs_all[:].bitcast(I32), 0)
-        nc.vector.memset(ws_raw[:].bitcast(I32), 0)
 
         nc.sync.dma_start(offs_t[:], offs)
-        nc.sync.dma_start(out=w_raw[:].bitcast(I32), in_=w1_words[0].bitcast(I32))
+        nc.scalar.dma_start(out=w_raw[:].bitcast(I32), in_=w1_words[0].bitcast(I32))
+        load_scale_rows([nc.scalar] * 4, ws_raw, w1_scales[0])
         nc.sync.dma_start(exp_t[:], exp_)
         nc.sync.dma_start(per_t[:], per)
-        nc.sync.dma_start(out=xw_all[:], in_=x_words[0].rearrange("p c r -> p (c r)").bitcast(I32))
-        load_scale_rows([nc.gpsimd] + [nc.scalar] * 3, xs_all, x_scales[0])
-        load_scale_rows([nc.scalar] * 4, ws_raw, w1_scales[0])
+        x_rows = x_words[0].rearrange("p c r -> p (c r)").bitcast(I32)
+        nc.sync.dma_start(out=xw_all[:, 0 : T // 2], in_=x_rows[:, 0 : T // 2])
+        load_scale_rows([nc.sync] * 4, xs_all, x_scales[0])
+        nc.sync.dma_start(out=xw_all[:, T // 2 : T], in_=x_rows[:, T // 2 : T])
 
         w1w = sb("w1w", [P, 2 * H], U8)
         w1s = sb("w1s", [P, H], U8)
-        w2w = sb("w2w", [P, 2 * H], U8)
-        w2s = sb("w2s", [P, H], U8)
         xs = [sb("xs%d" % h, [P, BANK], U8) for h in range(HALVES)]
         xw = [sb("xw%d" % h, [P, BANK], U32) for h in range(HALVES)]
         cols = BANK // 16
@@ -95,11 +96,14 @@ def tile_picked_yepitpr_dose_p_kernel(
         nc.gpsimd.dma_start(out=w_raw[:].bitcast(I32), in_=w2_words[0].bitcast(I32))
         load_scale_rows([nc.sync] * 4, ws_raw, w2_scales[0])
         mask_rows = mask.rearrange("(p t) s -> p t s", t=PACK)
-        mask_first = sb("xs_all", [P, S], F32)
-        mask_rest = sb("xw_all", [P, PACK - 1, S], F32)
-        nc.sync.dma_start(out=mask_first[:], in_=mask_rows[:, 0, :])
-        nc.sync.dma_start(out=mask_rest[:], in_=mask_rows[:, 1:PACK, :])
-        mask_t = [mask_first[:]] + [mask_rest[:, t, :] for t in range(PACK - 1)]
+        mask_head = reused.tile([P, PACK - 1, S], F32, name="mask_head", align_bytes=64, offset=0)
+        w2w = reused.tile([P, 2 * H], U8, name="w2w", align_bytes=64, offset=(PACK - 1) * S * 4)
+        w2s = reused.tile([P, H], U8, name="w2s", align_bytes=64, offset=(PACK - 1) * S * 4 + 2 * H)
+        mask_last = sb("xs_all", [P, S], F32)
+        nc.sync.dma_start(out=mask_head[:, 0, :], in_=mask_rows[:, 0, :])
+        nc.sync.dma_start(out=mask_head[:, 1 : PACK - 1, :], in_=mask_rows[:, 1 : PACK - 1, :])
+        nc.sync.dma_start(out=mask_last[:], in_=mask_rows[:, PACK - 1, :])
+        mask_t = [mask_head[:, t, :] for t in range(PACK - 1)] + [mask_last[:]]
 
         make_identity(nc, ident[:])
         minus_one = sb("minus_one", [P, P], F32)
@@ -165,9 +169,12 @@ def tile_picked_yepitpr_dose_p_kernel(
         for t in range(PACK):
             for h in range(HALVES):
                 sus = product(w2w, w2s, t, h)
-                nc.scalar.activation(
-                    half(susc[t], h).rearrange("p (d v) -> p d v", d=D), sus[:].rearrange("p (v d) -> p d v", d=D), ACT.Sigmoid
-                )
+                if t == PACK - 1:
+                    nc.scalar.activation(half(susc[t], h), sus[:], ACT.Sigmoid)
+                else:
+                    nc.scalar.activation(
+                        half(susc[t], h).rearrange("p (d v) -> p d v", d=D), sus[:].rearrange("p (v d) -> p d v", d=D), ACT.Sigmoid
+                    )
         for t in range(1, PACK):
             make_dose(t)
 
@@ -194,47 +201,45 @@ def tile_picked_yepitpr_dose_p_kernel(
         weight = sb("weight", [P, V], F32)
         nc.vector.tensor_scalar(weight[:], mxd[last][:], neg_unit[:, last : last + 1], None, ALU.mult)
 
-        for t in range(PACK - 1):
-            nc.scalar.activation(
-                recip[t][:].rearrange("p (h d v) -> p h v d", h=HALVES, d=D),
-                ln1p[t][:].rearrange("p (h v d) -> p h v d", h=HALVES, d=D),
-                ACT.Exp,
-                scale=-1.0,
-            )
-            nc.vector.scalar_tensor_tensor(
-                neg_haz[t][:].rearrange("p h d v -> p (h d v)"), recip[t][:], 1.0, susc[t][:], ALU.subtract, ALU.mult
-            )
+        for t in range(last):
             turned = bank(HALVES * t, V)
+            escape = bank(HALVES * t + 1, V)
             for h in range(HALVES):
+                nc.tensor.matmul(escape[:, P * h : P * (h + 1)], minus_one[:], ident[:], start=(h == 0), stop=False, is_transpose=True)
+            for h in range(HALVES):
+                nc.scalar.activation(
+                    half(recip[t], h).rearrange("p (d v) -> p v d", d=D), half(ln1p[t], h).rearrange("p (v d) -> p v d", d=D), ACT.Exp, scale=-1.0
+                )
+                nc.vector.scalar_tensor_tensor(
+                    neg_haz[t][:, h].rearrange("p d v -> p (d v)"), half(recip[t], h), 1.0, half(susc[t], h), ALU.subtract, ALU.mult
+                )
                 for d in range(D):
                     nc.tensor.matmul(
                         turned[:, P * h : P * (h + 1)], neg_haz[t][:, h, d, :], ident[:], start=(d == 0), stop=(d == D - 1), is_transpose=True
                     )
             escape_turned = sb("escape%d" % t, [P, V], F32)
             nc.scalar.activation(escape_turned[:], turned[:], ACT.Exp)
-            escape = bank(HALVES * t + 1, V)
             for h in range(HALVES):
                 cols_h = slice(P * h, P * (h + 1))
-                nc.tensor.matmul(escape[:, cols_h], minus_one[:], ident[:], start=True, stop=False, is_transpose=True)
-                nc.tensor.matmul(escape[:, cols_h], escape_turned[:, cols_h], ident[:], start=False, stop=True, is_transpose=True)
+                nc.tensor.matmul(escape[:, cols_h], escape_turned[:, cols_h], ident[:], start=False, stop=(h == HALVES - 1), is_transpose=True)
             nc.vector.scalar_tensor_tensor(group[t][:, 0:V], mxd[t][:], neg_unit[:, t : t + 1], escape[:], ALU.mult, ALU.mult)
 
-        t = PACK - 1
-        pair_sum = sb("pair_sum", [P, HALVES, 2, P], F32)
+        t = last
+        pair_sum = sb("pair_sum", [P, HALVES, P, 2], F32)
         neg_toth = sb("neg_toth", [P, HALVES, P], F32)
+        escape = sb("escape%d" % t, [P, HALVES, P], F32)
         for h in range(HALVES):
-            nc.scalar.activation(
-                half(recip[t], h).rearrange("p (d v) -> p v d", d=D), half(ln1p[t], h).rearrange("p (v d) -> p v d", d=D), ACT.Exp, scale=-1.0
-            )
+            haz_h = neg_haz[t][:, h].rearrange("p d v -> p (d v)")
+            nc.scalar.activation(half(recip[t], h), half(ln1p[t], h), ACT.Exp, scale=-1.0)
+            nc.vector.scalar_tensor_tensor(haz_h, half(recip[t], h), 1.0, half(susc[t], h), ALU.subtract, ALU.mult)
+            quads = haz_h.rearrange("p (v d) -> p v d", d=D)
+            nc.vector.tensor_tensor(pair_sum[:, h], quads[:, :, 0:2], quads[:, :, 2:4], ALU.add)
+            nc.vector.tensor_tensor(neg_toth[:, h], pair_sum[:, h, :, 0], pair_sum[:, h, :, 1], ALU.add)
+        for h in range(HALVES):
+            nc.scalar.activation(escape[:, h], neg_toth[:, h], ACT.Exp)
             nc.vector.scalar_tensor_tensor(
-                neg_haz[t][:, h].rearrange("p d v -> p (d v)"), half(recip[t], h), 1.0, half(susc[t], h), ALU.subtract, ALU.mult
+                group[t][:, P * h : P * (h + 1)], escape[:, h], 1.0, weight[:, P * h : P * (h + 1)], ALU.subtract, ALU.mult
             )
-        for h in range(HALVES):
-            nc.vector.tensor_tensor(pair_sum[:, h], neg_haz[t][:, h, 0:2, :], neg_haz[t][:, h, 2:4, :], ALU.add)
-        nc.vector.tensor_tensor(neg_toth[:], pair_sum[:, :, 0, :], pair_sum[:, :, 1, :], ALU.add)
-        escape = sb("escape%d" % t, [P, V], F32)
-        nc.scalar.activation(escape[:], neg_toth[:].rearrange("p h v -> p (h v)"), ACT.Exp)
-        nc.vector.scalar_tensor_tensor(group[t][:, 0:V], escape[:], 1.0, weight[:], ALU.subtract, ALU.mult)
 
         UH = U // 2
         planes = [sb("planes%d" % j, [P, PACK, UH], BF16) for j in range(2)]

@@ -18,29 +18,42 @@ ACT = mybir.ActivationFunctionType
 ALU = mybir.AluOpType
 
 P = 128
-PACK = 4
+PLANES = 4
+LAST = PLANES - 1
+QUADRANTS = 4
 BANK = 512
 HALVES = S // BANK
+LIST_ROWS = 16
+PEOPLE = U // 2
 LN_FLOOR = 2.0**-63
+FIRST_SHARED_PLANE = 2
 
 
-def load_scale_rows(queues, plane, rows):
-    for q, queue in enumerate(queues):
+def load_scale_rows(queue, plane, rows):
+    for q in range(QUADRANTS):
         queue.dma_start(out=plane[32 * q : 32 * q + 4].bitcast(I32), in_=rows[4 * q : 4 * q + 4, :].bitcast(I32))
 
 
 def deal_words(nc, dealt, raw):
     nc.vector.tensor_copy(
-        out=dealt[:].rearrange("p (t m b) -> p t m b", t=PACK, b=2),
-        in_=raw[:].rearrange("p (m t b) -> p t m b", t=PACK, b=2),
+        out=dealt[:].rearrange("p (t m b) -> p t m b", t=PLANES, b=2),
+        in_=raw[:].rearrange("p (m t b) -> p t m b", t=PLANES, b=2),
     )
 
 
 def deal_scales(nc, dealt, raw):
     nc.vector.tensor_copy(
-        out=dealt[:].rearrange("p (t m) -> p t m", t=PACK),
-        in_=raw[:].rearrange("p (m t) -> p t m", t=PACK),
+        out=dealt[:].rearrange("p (t m) -> p t m", t=PLANES),
+        in_=raw[:].rearrange("p (m t) -> p t m", t=PLANES),
     )
+
+
+def half(ap, h):
+    return ap[:, BANK * h : BANK * (h + 1)]
+
+
+def entries(list_tile, first, count):
+    return list_tile[:, first // LIST_ROWS : (first + count) // LIST_ROWS]
 
 
 def tile_picked_yepitpr_dose_p_kernel(
@@ -52,63 +65,63 @@ def tile_picked_yepitpr_dose_p_kernel(
         reused = ctx.enter_context(tc.tile_pool(name="reused", bufs=1))
         psum = ctx.enter_context(tc.psum_pool(name="psum", bufs=1))
 
-        def sb(name, shape, dtype):
-            return keep.tile(shape, dtype, name=name, align_bytes=64)
+        def sb(slot, shape, dtype):
+            return keep.tile(shape, dtype, name=slot, align_bytes=64)
 
         def bank(b, width=BANK):
             return psum.tile([P, width], F32, name="bank%d" % b)
 
-        offs_t = sb("offs_t", [P, S // 16], U16)
-        exp_t = sb("exp_t", [P, S // 16], U16)
-        per_t = sb("per_t", [P, U // 16], U16)
+        offs_t = sb("offs_t", [P, S // LIST_ROWS], U16)
+        exp_t = sb("exp_t", [P, S // LIST_ROWS], U16)
+        per_t = sb("per_t", [P, U // LIST_ROWS], U16)
         xw_all = reused.tile([P, T], I32, name="xw_all", align_bytes=64, offset=0)
         xs_all = sb("xs_all", [P, T], U8)
         w_raw = sb("w_raw", [P, 2 * H], U8)
         ws_raw = sb("ws_raw", [P, H], U8)
         ident = sb("ident", [P, P], F32)
-        unit_t = sb("unit_t", [P, PACK], F32)
+        unit_t = sb("unit_t", [P, PLANES], F32)
 
         nc.gpsimd.memset(ws_raw[:].bitcast(I32), 0)
         nc.vector.memset(xs_all[:].bitcast(I32), 0)
 
         nc.sync.dma_start(offs_t[:], offs)
         nc.scalar.dma_start(out=w_raw[:].bitcast(I32), in_=w1_words[0].bitcast(I32))
-        load_scale_rows([nc.scalar] * 4, ws_raw, w1_scales[0])
+        load_scale_rows(nc.scalar, ws_raw, w1_scales[0])
         nc.sync.dma_start(exp_t[:], exp_)
         nc.sync.dma_start(per_t[:], per)
         x_rows = x_words[0].rearrange("p c r -> p (c r)").bitcast(I32)
         nc.sync.dma_start(out=xw_all[:, 0 : T // 2], in_=x_rows[:, 0 : T // 2])
-        load_scale_rows([nc.sync] * 4, xs_all, x_scales[0])
+        load_scale_rows(nc.sync, xs_all, x_scales[0])
         nc.sync.dma_start(out=xw_all[:, T // 2 : T], in_=x_rows[:, T // 2 : T])
 
         w1w = sb("w1w", [P, 2 * H], U8)
         w1s = sb("w1s", [P, H], U8)
         xs = [sb("xs%d" % h, [P, BANK], U8) for h in range(HALVES)]
         xw = [sb("xw%d" % h, [P, BANK], U32) for h in range(HALVES)]
-        cols = BANK // 16
         deal_words(nc, w1w, w_raw)
         deal_scales(nc, w1s, ws_raw)
         for h in range(HALVES):
-            picked = offs_t[:, h * cols : (h + 1) * cols]
+            picked = entries(offs_t, BANK * h, BANK)
             nc.vector.tensor_copy(xs[h][:], xs_all[:].indirect(picked))
             nc.vector.tensor_copy(xw[h][:], xw_all[:].bitcast(U32).indirect(picked))
 
         nc.gpsimd.dma_start(out=w_raw[:].bitcast(I32), in_=w2_words[0].bitcast(I32))
-        load_scale_rows([nc.sync] * 4, ws_raw, w2_scales[0])
-        mask_rows = mask.rearrange("(p t) s -> p t s", t=PACK)
-        mask_head = reused.tile([P, PACK - 1, S], F32, name="mask_head", align_bytes=64, offset=0)
-        w2w = reused.tile([P, 2 * H], U8, name="w2w", align_bytes=64, offset=(PACK - 1) * S * 4)
-        w2s = reused.tile([P, H], U8, name="w2s", align_bytes=64, offset=(PACK - 1) * S * 4 + 2 * H)
+        load_scale_rows(nc.sync, ws_raw, w2_scales[0])
+        mask_rows = mask.rearrange("(p t) s -> p t s", t=PLANES)
+        mask_head_bytes = LAST * S * 4
+        mask_head = reused.tile([P, LAST, S], F32, name="mask_head", align_bytes=64, offset=0)
+        w2w = reused.tile([P, 2 * H], U8, name="w2w", align_bytes=64, offset=mask_head_bytes)
+        w2s = reused.tile([P, H], U8, name="w2s", align_bytes=64, offset=mask_head_bytes + 2 * H)
         mask_last = sb("xs_all", [P, S], F32)
         nc.sync.dma_start(out=mask_head[:, 0, :], in_=mask_rows[:, 0, :])
-        nc.sync.dma_start(out=mask_head[:, 1 : PACK - 1, :], in_=mask_rows[:, 1 : PACK - 1, :])
-        nc.sync.dma_start(out=mask_last[:], in_=mask_rows[:, PACK - 1, :])
-        mask_t = [mask_head[:, t, :] for t in range(PACK - 1)] + [mask_last[:]]
+        nc.sync.dma_start(out=mask_head[:, 1:LAST, :], in_=mask_rows[:, 1:LAST, :])
+        nc.sync.dma_start(out=mask_last[:], in_=mask_rows[:, LAST, :])
+        mask_t = [mask_head[:, t, :] for t in range(LAST)] + [mask_last[:]]
 
         make_identity(nc, ident[:])
         minus_one = sb("minus_one", [P, P], F32)
         nc.gpsimd.memset(minus_one[:], -1.0)
-        nc.gpsimd.dma_start(out=unit_t[:], in_=unit.rearrange("(p t) o -> p (t o)", t=PACK))
+        nc.gpsimd.dma_start(out=unit_t[:], in_=unit.rearrange("(p t) o -> p (t o)", t=PLANES))
 
         def product(words, scales, t, h):
             acc = bank(HALVES * t + h)
@@ -123,42 +136,42 @@ def tile_picked_yepitpr_dose_p_kernel(
             )
             return acc
 
-        def half(tile, h):
-            return tile[:, BANK * h : BANK * (h + 1)]
+        def add_transposed(acc, block, start, stop):
+            nc.tensor.matmul(acc, block, ident[:], start=start, stop=stop, is_transpose=True)
 
         inf = {}
-        sneg = [sb("sneg%d" % t, [P, S], F32) for t in range(PACK)]
+        sig_neg = [sb("wide_a%d" % t, [P, S], F32) for t in range(PLANES)]
         for h in range(HALVES):
-            for t in range(PACK):
+            for t in range(PLANES):
                 inf[t, h] = product(w1w, w1s, t, h)
-                nc.scalar.activation(half(sneg[t], h), inf[t, h][:], ACT.Sigmoid, scale=-1.0)
+                nc.scalar.activation(half(sig_neg[t], h), inf[t, h][:], ACT.Sigmoid, scale=-1.0)
 
         deal_words(nc, w2w, w_raw)
         deal_scales(nc, w2s, ws_raw)
         w3w = w_raw[:, 0 : 2 * N]
         w3s = ws_raw[:, 0:N]
         nc.sync.dma_start(out=w3w.bitcast(I32), in_=w3_words[0].bitcast(I32))
-        load_scale_rows([nc.sync] * 4, w3s, w3_scales[0])
-        neg_unit = sb("neg_unit", [P, PACK], F32)
+        load_scale_rows(nc.sync, w3s, w3_scales[0])
+        neg_unit = sb("neg_unit", [P, PLANES], F32)
         nc.vector.tensor_scalar(neg_unit[:], unit_t[:], -1.0, None, ALU.mult)
 
-        lsig = [sb("lsig%d" % t, [P, S], F32) for t in range(PACK)]
-        load = [sb("load%d" % t, [P, S], F32) for t in range(PACK)]
-        dose = [sb("dose%d" % t, [P, S], F32) for t in range(PACK)]
-        susc = [sb("susc%d" % t, [P, S], F32) for t in range(PACK)]
+        ln_sig = [sb("wide_b%d" % t, [P, S], F32) for t in range(PLANES)]
+        load = [sb("wide_c%d" % t, [P, S], F32) for t in range(PLANES)]
+        dose = [sb("dose%d" % t, [P, S], F32) for t in range(PLANES)]
+        susc = [sb("susc%d" % t, [P, S], F32) for t in range(PLANES)]
         for h in range(HALVES):
-            nc.scalar.activation(half(lsig[0], h), half(sneg[0], h), ACT.Ln, bias=LN_FLOOR)
-        for t in range(1, PACK):
-            nc.scalar.activation(lsig[t][:], sneg[t][:], ACT.Ln, bias=LN_FLOOR)
+            nc.scalar.activation(half(ln_sig[0], h), half(sig_neg[0], h), ACT.Ln, bias=LN_FLOOR)
+        for t in range(1, PLANES):
+            nc.scalar.activation(ln_sig[t][:], sig_neg[t][:], ACT.Ln, bias=LN_FLOOR)
 
         def make_load(t):
             for h in range(HALVES):
-                nc.vector.scalar_tensor_tensor(half(load[t], h), half(lsig[t], h), -1.0, inf[t, h][:], ALU.mult, ALU.max)
+                nc.vector.scalar_tensor_tensor(half(load[t], h), half(ln_sig[t], h), -1.0, inf[t, h][:], ALU.mult, ALU.max)
 
         def make_dose(t):
             for h in range(HALVES):
                 nc.vector.tensor_tensor(
-                    half(dose[t], h), load[t][:].indirect(exp_t[:, h * cols : (h + 1) * cols]), half(mask_t[t], h), ALU.mult
+                    half(dose[t], h), load[t][:].indirect(entries(exp_t, BANK * h, BANK)), half(mask_t[t], h), ALU.mult
                 )
 
         make_load(0)
@@ -166,106 +179,113 @@ def tile_picked_yepitpr_dose_p_kernel(
         make_dose(0)
         make_load(2)
         make_load(3)
-        for t in range(PACK):
+
+        for t in range(PLANES):
             for h in range(HALVES):
                 sus = product(w2w, w2s, t, h)
-                if t == PACK - 1:
+                if t == LAST:
                     nc.scalar.activation(half(susc[t], h), sus[:], ACT.Sigmoid)
                 else:
                     nc.scalar.activation(
                         half(susc[t], h).rearrange("p (d v) -> p d v", d=D), sus[:].rearrange("p (v d) -> p d v", d=D), ACT.Sigmoid
                     )
-        for t in range(1, PACK):
+        for t in range(1, PLANES):
             make_dose(t)
 
-        ln1p = [sb("lsig%d" % t, [P, S], F32) for t in range(PACK)]
-        for t in range(PACK):
-            nc.scalar.activation(ln1p[t][:], dose[t][:], ACT.Ln, bias=1.0)
+        ln_dose1 = [sb("wide_b%d" % t, [P, S], F32) for t in range(PLANES)]
+        for t in range(PLANES):
+            nc.scalar.activation(ln_dose1[t][:], dose[t][:], ACT.Ln, bias=1.0)
 
-        group = [sb("group%d" % t, [P, 3 * V], F32) for t in range(PACK)]
-        mxd = [sb("mxd%d" % t, [P, V], F32) for t in range(PACK)]
-        for pair in ((0, 1), (2, 3)):
-            for t in pair:
+        group = [sb("group%d" % t, [P, 3 * V], F32) for t in range(PLANES)]
+        mxd = [sb("mxd%d" % t, [P, V], F32) for t in range(PLANES)]
+        for first in range(0, PLANES, 2):
+            for t in (first, first + 1):
                 quads = dose[t][:].rearrange("p (v d) -> p v d", d=D)
                 nc.vector.tensor_tensor(
                     group[t][:, V : 3 * V].rearrange("p (v d) -> p v d", d=2), quads[:, :, 0:2], quads[:, :, 2:4], ALU.max
                 )
-            for t in pair:
+            for t in (first, first + 1):
                 pairs = group[t][:, V : 3 * V].rearrange("p (v d) -> p v d", d=2)
                 nc.vector.tensor_tensor(mxd[t][:], pairs[:, :, 0], pairs[:, :, 1], ALU.max)
 
-        recip = [sb("sneg%d" % t, [P, S], F32) for t in range(PACK)]
-        neg_haz = [sb("load%d" % t, [P, HALVES, D, P], F32) for t in range(PACK)]
+        recip = [sb("wide_a%d" % t, [P, S], F32) for t in range(PLANES)]
+        neg_haz = [sb("wide_c%d" % t, [P, HALVES, D, P], F32) for t in range(PLANES)]
+        neg_weight = sb("neg_weight", [P, V], F32)
+        nc.vector.tensor_scalar(neg_weight[:], mxd[LAST][:], neg_unit[:, LAST : LAST + 1], None, ALU.mult)
 
-        last = PACK - 1
-        weight = sb("weight", [P, V], F32)
-        nc.vector.tensor_scalar(weight[:], mxd[last][:], neg_unit[:, last : last + 1], None, ALU.mult)
-
-        for t in range(last):
-            turned = bank(HALVES * t, V)
-            escape = bank(HALVES * t + 1, V)
+        for t in range(LAST):
+            neg_toth_turned = bank(HALVES * t, V)
+            neg_pinf = bank(HALVES * t + 1, V)
             for h in range(HALVES):
-                nc.tensor.matmul(escape[:, P * h : P * (h + 1)], minus_one[:], ident[:], start=(h == 0), stop=False, is_transpose=True)
+                add_transposed(neg_pinf[:, P * h : P * (h + 1)], minus_one[:], h == 0, False)
             for h in range(HALVES):
                 nc.scalar.activation(
-                    half(recip[t], h).rearrange("p (d v) -> p v d", d=D), half(ln1p[t], h).rearrange("p (v d) -> p v d", d=D), ACT.Exp, scale=-1.0
+                    half(recip[t], h).rearrange("p (d v) -> p v d", d=D),
+                    half(ln_dose1[t], h).rearrange("p (v d) -> p v d", d=D),
+                    ACT.Exp,
+                    scale=-1.0,
                 )
                 nc.vector.scalar_tensor_tensor(
                     neg_haz[t][:, h].rearrange("p d v -> p (d v)"), half(recip[t], h), 1.0, half(susc[t], h), ALU.subtract, ALU.mult
                 )
                 for d in range(D):
-                    nc.tensor.matmul(
-                        turned[:, P * h : P * (h + 1)], neg_haz[t][:, h, d, :], ident[:], start=(d == 0), stop=(d == D - 1), is_transpose=True
-                    )
+                    add_transposed(neg_toth_turned[:, P * h : P * (h + 1)], neg_haz[t][:, h, d, :], d == 0, d == D - 1)
             escape_turned = sb("escape%d" % t, [P, V], F32)
-            nc.scalar.activation(escape_turned[:], turned[:], ACT.Exp)
+            nc.scalar.activation(escape_turned[:], neg_toth_turned[:], ACT.Exp)
             for h in range(HALVES):
-                cols_h = slice(P * h, P * (h + 1))
-                nc.tensor.matmul(escape[:, cols_h], escape_turned[:, cols_h], ident[:], start=False, stop=(h == HALVES - 1), is_transpose=True)
-            nc.vector.scalar_tensor_tensor(group[t][:, 0:V], mxd[t][:], neg_unit[:, t : t + 1], escape[:], ALU.mult, ALU.mult)
+                groups = slice(P * h, P * (h + 1))
+                add_transposed(neg_pinf[:, groups], escape_turned[:, groups], False, h == HALVES - 1)
+            nc.vector.scalar_tensor_tensor(group[t][:, 0:V], mxd[t][:], neg_unit[:, t : t + 1], neg_pinf[:], ALU.mult, ALU.mult)
 
-        t = last
-        pair_sum = sb("pair_sum", [P, HALVES, P, 2], F32)
         neg_toth = sb("neg_toth", [P, HALVES, P], F32)
-        escape = sb("escape%d" % t, [P, HALVES, P], F32)
+        escape = sb("escape%d" % LAST, [P, HALVES, P], F32)
         for h in range(HALVES):
-            haz_h = neg_haz[t][:, h].rearrange("p d v -> p (d v)")
-            nc.scalar.activation(half(recip[t], h), half(ln1p[t], h), ACT.Exp, scale=-1.0)
-            nc.vector.scalar_tensor_tensor(haz_h, half(recip[t], h), 1.0, half(susc[t], h), ALU.subtract, ALU.mult)
-            quads = haz_h.rearrange("p (v d) -> p v d", d=D)
-            nc.vector.tensor_tensor(pair_sum[:, h], quads[:, :, 0:2], quads[:, :, 2:4], ALU.add)
-            nc.vector.tensor_tensor(neg_toth[:, h], pair_sum[:, h, :, 0], pair_sum[:, h, :, 1], ALU.add)
+            neg_haz_half = neg_haz[LAST][:, h].rearrange("p a b -> p (a b)")
+            nc.scalar.activation(half(recip[LAST], h), half(ln_dose1[LAST], h), ACT.Exp, scale=-1.0)
+            nc.vector.scalar_tensor_tensor(neg_haz_half, half(recip[LAST], h), 1.0, half(susc[LAST], h), ALU.subtract, ALU.mult)
+            nc.vector.tensor_reduce(neg_toth[:, h], neg_haz_half.rearrange("p (v d) -> p v d", d=D), mybir.AxisListType.X, ALU.add)
         for h in range(HALVES):
+            groups = slice(P * h, P * (h + 1))
             nc.scalar.activation(escape[:, h], neg_toth[:, h], ACT.Exp)
-            nc.vector.scalar_tensor_tensor(
-                group[t][:, P * h : P * (h + 1)], escape[:, h], 1.0, weight[:, P * h : P * (h + 1)], ALU.subtract, ALU.mult
-            )
+            nc.vector.scalar_tensor_tensor(group[LAST][:, groups], escape[:, h], 1.0, neg_weight[:, groups], ALU.subtract, ALU.mult)
 
-        UH = U // 2
-        planes = [sb("planes%d" % j, [P, PACK, UH], BF16) for j in range(2)]
-        for t in range(PACK):
+        hid_planes = [sb("hid_planes%d" % j, [P, PLANES, PEOPLE], BF16) for j in range(2)]
+        for t in range(PLANES):
             for j in range(2):
-                people = group[t][:].indirect(per_t[:, j * UH // 16 : (j + 1) * UH // 16])
-                if t >= 2 and j == 0:
-                    nc.vector.tensor_copy(planes[j][:, t, :], people)
+                looked_up = group[t][:].indirect(entries(per_t, PEOPLE * j, PEOPLE))
+                if t >= FIRST_SHARED_PLANE and j == 0:
+                    nc.vector.tensor_copy(hid_planes[j][:, t, :], looked_up)
                 else:
-                    nc.scalar.activation(planes[j][:, t, :], people, ACT.Copy)
+                    nc.scalar.activation(hid_planes[j][:, t, :], looked_up, ACT.Copy)
 
-        hid = [sb("hid%d" % j, [P, UH, PACK], BF16) for j in range(2)]
-        hq = [sb("hq%d" % j, [P, UH], U32) for j in range(2)]
-        hs = [sb("hs%d" % j, [P, UH], U8) for j in range(2)]
-        for j in range(2):
-            nc.vector.tensor_copy(
-                hid[j][:].rearrange("p (c i) t -> p c t i", i=4), planes[j][:].rearrange("p t (c i) -> p c t i", i=4)
+        hid = [sb("hid%d" % j, [P, PEOPLE, PLANES], BF16) for j in range(2)]
+        hid_words = [sb("hid_words%d" % j, [P, PEOPLE], U32) for j in range(2)]
+        hid_scales = [sb("hid_scales%d" % j, [P, PEOPLE], U8) for j in range(2)]
+
+        def interleave(copy, j, people):
+            copy(
+                hid[j][:, people, :].rearrange("p (c i) t -> p c t i", i=4),
+                hid_planes[j][:, :, people].rearrange("p t (c i) -> p c t i", i=4),
             )
+
+        interleave(nc.vector.tensor_copy, 0, slice(0, PEOPLE))
+        interleave(nc.vector.tensor_copy, 1, slice(0, PEOPLE // 2))
+        interleave(nc.scalar.copy, 1, slice(PEOPLE // 2, PEOPLE))
         for j in range(2):
-            nc.vector.quantize_mx(out=hq[j][:].bitcast(FP8X4), scales=hs[j][:], in_=hid[j][:].rearrange("p r t -> p (r t)"))
+            nc.vector.quantize_mx(
+                out=hid_words[j][:].bitcast(FP8X4), scales=hid_scales[j][:], in_=hid[j][:].rearrange("p r t -> p (r t)")
+            )
         for j, queue in enumerate((nc.sync, nc.scalar)):
-            acc = bank(HALVES * (PACK - 1) + j, UH)
+            acc = bank(HALVES * LAST + j, PEOPLE)
             nc.tensor.matmul_mx(
-                out=acc[:], lhsT=w3w.bitcast(FP4X4), lhsT_scale=w3s, rhs=hq[j][:].bitcast(FP8X4), rhs_scale=hs[j][:],
-                start=True, stop=True,
+                out=acc[:],
+                lhsT=w3w.bitcast(FP4X4),
+                lhsT_scale=w3s,
+                rhs=hid_words[j][:].bitcast(FP8X4),
+                rhs_scale=hid_scales[j][:],
+                start=True,
+                stop=True,
             )
-            res = sb("res%d" % j, [P, UH], F32)
-            nc.scalar.copy(res[:], acc[:])
-            queue.dma_start(out=out[:, j * UH : (j + 1) * UH], in_=res[:])
+            result = sb("result%d" % j, [P, PEOPLE], F32)
+            nc.scalar.copy(result[:], acc[:])
+            queue.dma_start(out=out[:, PEOPLE * j : PEOPLE * (j + 1)], in_=result[:])

from contextlib import ExitStack

import concourse.mybir as mybir
from concourse.masks import make_identity

K, T, S, D, N, H, V, U = 512, 4096, 1024, 4, 128, 512, 256, 512
FLOPS = 2 * K * H * S * 2 + 2 * H * N * U

F32 = mybir.dt.float32
BF16 = mybir.dt.bfloat16
I32 = mybir.dt.int32
U32 = mybir.dt.uint32
U16 = mybir.dt.uint16
U8 = mybir.dt.uint8
FP8X4 = mybir.dt.float8_e4m3fn_x4
FP4X4 = mybir.dt.float4_e2m1fn_x4
ACT = mybir.ActivationFunctionType
ALU = mybir.AluOpType

P = 128
PLANES = 4
LAST = PLANES - 1
QUADRANTS = 4
BANK = 512
HALVES = S // BANK
LIST_ROWS = 16
PEOPLE = U // 2
LN_FLOOR = 2.0**-63
FIRST_SHARED_PLANE = 2


def load_scale_rows(queue, plane, rows):
    for q in range(QUADRANTS):
        queue.dma_start(out=plane[32 * q : 32 * q + 4].bitcast(I32), in_=rows[4 * q : 4 * q + 4, :].bitcast(I32))


def deal_words(nc, dealt, raw):
    nc.vector.tensor_copy(
        out=dealt[:].rearrange("p (t m b) -> p t m b", t=PLANES, b=2),
        in_=raw[:].rearrange("p (m t b) -> p t m b", t=PLANES, b=2),
    )


def deal_scales(nc, dealt, raw):
    nc.vector.tensor_copy(
        out=dealt[:].rearrange("p (t m) -> p t m", t=PLANES),
        in_=raw[:].rearrange("p (m t) -> p t m", t=PLANES),
    )


def half(ap, h):
    return ap[:, BANK * h : BANK * (h + 1)]


def entries(list_tile, first, count):
    return list_tile[:, first // LIST_ROWS : (first + count) // LIST_ROWS]


def tile_picked_yepitpr_dose_p_kernel(
    tc, x_words, x_scales, w1_words, w1_scales, w2_words, w2_scales, mask, unit, w3_words, w3_scales, offs, exp_, per, out
):
    nc = tc.nc
    with ExitStack() as ctx:
        keep = ctx.enter_context(tc.tile_pool(name="keep", bufs=1))
        reused = ctx.enter_context(tc.tile_pool(name="reused", bufs=1))
        psum = ctx.enter_context(tc.psum_pool(name="psum", bufs=1))

        def sb(slot, shape, dtype):
            return keep.tile(shape, dtype, name=slot, align_bytes=64)

        def bank(b, width=BANK):
            return psum.tile([P, width], F32, name="bank%d" % b)

        offs_t = sb("offs_t", [P, S // LIST_ROWS], U16)
        exp_t = sb("exp_t", [P, S // LIST_ROWS], U16)
        per_t = sb("per_t", [P, U // LIST_ROWS], U16)
        xw_all = reused.tile([P, T], I32, name="xw_all", align_bytes=64, offset=0)
        xs_all = sb("xs_all", [P, T], U8)
        w_raw = sb("w_raw", [P, 2 * H], U8)
        ws_raw = sb("ws_raw", [P, H], U8)
        ident = sb("ident", [P, P], F32)
        unit_t = sb("unit_t", [P, PLANES], F32)

        nc.gpsimd.memset(ws_raw[:].bitcast(I32), 0)
        nc.vector.memset(xs_all[:].bitcast(I32), 0)

        nc.sync.dma_start(offs_t[:], offs)
        nc.scalar.dma_start(out=w_raw[:].bitcast(I32), in_=w1_words[0].bitcast(I32))
        load_scale_rows(nc.scalar, ws_raw, w1_scales[0])
        nc.sync.dma_start(exp_t[:], exp_)
        nc.sync.dma_start(per_t[:], per)
        x_rows = x_words[0].rearrange("p c r -> p (c r)").bitcast(I32)
        nc.sync.dma_start(out=xw_all[:, 0 : T // 2], in_=x_rows[:, 0 : T // 2])
        load_scale_rows(nc.sync, xs_all, x_scales[0])
        nc.sync.dma_start(out=xw_all[:, T // 2 : T], in_=x_rows[:, T // 2 : T])

        w1w = sb("w1w", [P, 2 * H], U8)
        w1s = sb("w1s", [P, H], U8)
        xs = [sb("xs%d" % h, [P, BANK], U8) for h in range(HALVES)]
        xw = [sb("xw%d" % h, [P, BANK], U32) for h in range(HALVES)]
        deal_words(nc, w1w, w_raw)
        deal_scales(nc, w1s, ws_raw)
        for h in range(HALVES):
            picked = entries(offs_t, BANK * h, BANK)
            nc.vector.tensor_copy(xs[h][:], xs_all[:].indirect(picked))
            nc.vector.tensor_copy(xw[h][:], xw_all[:].bitcast(U32).indirect(picked))

        nc.gpsimd.dma_start(out=w_raw[:].bitcast(I32), in_=w2_words[0].bitcast(I32))
        load_scale_rows(nc.sync, ws_raw, w2_scales[0])
        mask_rows = mask.rearrange("(p t) s -> p t s", t=PLANES)
        mask_head_bytes = LAST * S * 4
        mask_head = reused.tile([P, LAST, S], F32, name="mask_head", align_bytes=64, offset=0)
        w2w = reused.tile([P, 2 * H], U8, name="w2w", align_bytes=64, offset=mask_head_bytes)
        w2s = reused.tile([P, H], U8, name="w2s", align_bytes=64, offset=mask_head_bytes + 2 * H)
        mask_last = sb("xs_all", [P, S], F32)
        nc.sync.dma_start(out=mask_head[:, 0, :], in_=mask_rows[:, 0, :])
        nc.sync.dma_start(out=mask_head[:, 1:LAST, :], in_=mask_rows[:, 1:LAST, :])
        nc.sync.dma_start(out=mask_last[:], in_=mask_rows[:, LAST, :])
        mask_t = [mask_head[:, t, :] for t in range(LAST)] + [mask_last[:]]

        make_identity(nc, ident[:])
        minus_one = sb("minus_one", [P, P], F32)
        nc.gpsimd.memset(minus_one[:], -1.0)
        nc.gpsimd.dma_start(out=unit_t[:], in_=unit.rearrange("(p t) o -> p (t o)", t=PLANES))

        def product(words, scales, t, h):
            acc = bank(HALVES * t + h)
            nc.tensor.matmul_mx(
                out=acc[:],
                lhsT=words[:, 2 * P * t : 2 * P * (t + 1)].bitcast(FP4X4),
                lhsT_scale=scales[:, P * t : P * (t + 1)],
                rhs=xw[h][:].bitcast(FP8X4),
                rhs_scale=xs[h][:],
                start=True,
                stop=True,
            )
            return acc

        def add_transposed(acc, block, start, stop):
            nc.tensor.matmul(acc, block, ident[:], start=start, stop=stop, is_transpose=True)

        inf = {}
        sig_neg = [sb("wide_a%d" % t, [P, S], F32) for t in range(PLANES)]
        for h in range(HALVES):
            for t in range(PLANES):
                inf[t, h] = product(w1w, w1s, t, h)
                nc.scalar.activation(half(sig_neg[t], h), inf[t, h][:], ACT.Sigmoid, scale=-1.0)

        deal_words(nc, w2w, w_raw)
        deal_scales(nc, w2s, ws_raw)
        w3w = w_raw[:, 0 : 2 * N]
        w3s = ws_raw[:, 0:N]
        nc.sync.dma_start(out=w3w.bitcast(I32), in_=w3_words[0].bitcast(I32))
        load_scale_rows(nc.sync, w3s, w3_scales[0])
        neg_unit = sb("neg_unit", [P, PLANES], F32)
        nc.vector.tensor_scalar(neg_unit[:], unit_t[:], -1.0, None, ALU.mult)

        ln_sig = [sb("wide_b%d" % t, [P, S], F32) for t in range(PLANES)]
        load = [sb("wide_c%d" % t, [P, S], F32) for t in range(PLANES)]
        dose = [sb("dose%d" % t, [P, S], F32) for t in range(PLANES)]
        susc = [sb("susc%d" % t, [P, S], F32) for t in range(PLANES)]
        for h in range(HALVES):
            nc.scalar.activation(half(ln_sig[0], h), half(sig_neg[0], h), ACT.Ln, bias=LN_FLOOR)
        for t in range(1, PLANES):
            nc.scalar.activation(ln_sig[t][:], sig_neg[t][:], ACT.Ln, bias=LN_FLOOR)

        def make_load(t):
            for h in range(HALVES):
                nc.vector.scalar_tensor_tensor(half(load[t], h), half(ln_sig[t], h), -1.0, inf[t, h][:], ALU.mult, ALU.max)

        def make_dose(t):
            for h in range(HALVES):
                nc.vector.tensor_tensor(
                    half(dose[t], h), load[t][:].indirect(entries(exp_t, BANK * h, BANK)), half(mask_t[t], h), ALU.mult
                )

        make_load(0)
        make_load(1)
        make_dose(0)
        make_load(2)
        make_load(3)

        for t in range(PLANES):
            for h in range(HALVES):
                sus = product(w2w, w2s, t, h)
                if t == LAST:
                    nc.scalar.activation(half(susc[t], h), sus[:], ACT.Sigmoid)
                else:
                    nc.scalar.activation(
                        half(susc[t], h).rearrange("p (d v) -> p d v", d=D), sus[:].rearrange("p (v d) -> p d v", d=D), ACT.Sigmoid
                    )
        for t in range(1, PLANES):
            make_dose(t)

        ln_dose1 = [sb("wide_b%d" % t, [P, S], F32) for t in range(PLANES)]
        for t in range(PLANES):
            nc.scalar.activation(ln_dose1[t][:], dose[t][:], ACT.Ln, bias=1.0)

        group = [sb("group%d" % t, [P, 3 * V], F32) for t in range(PLANES)]
        mxd = [sb("mxd%d" % t, [P, V], F32) for t in range(PLANES)]
        for first in range(0, PLANES, 2):
            for t in (first, first + 1):
                quads = dose[t][:].rearrange("p (v d) -> p v d", d=D)
                nc.vector.tensor_tensor(
                    group[t][:, V : 3 * V].rearrange("p (v d) -> p v d", d=2), quads[:, :, 0:2], quads[:, :, 2:4], ALU.max
                )
            for t in (first, first + 1):
                pairs = group[t][:, V : 3 * V].rearrange("p (v d) -> p v d", d=2)
                nc.vector.tensor_tensor(mxd[t][:], pairs[:, :, 0], pairs[:, :, 1], ALU.max)

        recip = [sb("wide_a%d" % t, [P, S], F32) for t in range(PLANES)]
        neg_haz = [sb("wide_c%d" % t, [P, HALVES, D, P], F32) for t in range(PLANES)]
        neg_weight = sb("neg_weight", [P, V], F32)
        nc.vector.tensor_scalar(neg_weight[:], mxd[LAST][:], neg_unit[:, LAST : LAST + 1], None, ALU.mult)

        for t in range(LAST):
            neg_toth_turned = bank(HALVES * t, V)
            neg_pinf = bank(HALVES * t + 1, V)
            for h in range(HALVES):
                add_transposed(neg_pinf[:, P * h : P * (h + 1)], minus_one[:], h == 0, False)
            for h in range(HALVES):
                nc.scalar.activation(
                    half(recip[t], h).rearrange("p (d v) -> p v d", d=D),
                    half(ln_dose1[t], h).rearrange("p (v d) -> p v d", d=D),
                    ACT.Exp,
                    scale=-1.0,
                )
                nc.vector.scalar_tensor_tensor(
                    neg_haz[t][:, h].rearrange("p d v -> p (d v)"), half(recip[t], h), 1.0, half(susc[t], h), ALU.subtract, ALU.mult
                )
                for d in range(D):
                    add_transposed(neg_toth_turned[:, P * h : P * (h + 1)], neg_haz[t][:, h, d, :], d == 0, d == D - 1)
            escape_turned = sb("escape%d" % t, [P, V], F32)
            nc.scalar.activation(escape_turned[:], neg_toth_turned[:], ACT.Exp)
            for h in range(HALVES):
                groups = slice(P * h, P * (h + 1))
                add_transposed(neg_pinf[:, groups], escape_turned[:, groups], False, h == HALVES - 1)
            nc.vector.scalar_tensor_tensor(group[t][:, 0:V], mxd[t][:], neg_unit[:, t : t + 1], neg_pinf[:], ALU.mult, ALU.mult)

        neg_toth = sb("neg_toth", [P, HALVES, P], F32)
        escape = sb("escape%d" % LAST, [P, HALVES, P], F32)
        for h in range(HALVES):
            neg_haz_half = neg_haz[LAST][:, h].rearrange("p a b -> p (a b)")
            nc.scalar.activation(half(recip[LAST], h), half(ln_dose1[LAST], h), ACT.Exp, scale=-1.0)
            nc.vector.scalar_tensor_tensor(neg_haz_half, half(recip[LAST], h), 1.0, half(susc[LAST], h), ALU.subtract, ALU.mult)
            nc.vector.tensor_reduce(neg_toth[:, h], neg_haz_half.rearrange("p (v d) -> p v d", d=D), mybir.AxisListType.X, ALU.add)
        for h in range(HALVES):
            groups = slice(P * h, P * (h + 1))
            nc.scalar.activation(escape[:, h], neg_toth[:, h], ACT.Exp)
            nc.vector.scalar_tensor_tensor(group[LAST][:, groups], escape[:, h], 1.0, neg_weight[:, groups], ALU.subtract, ALU.mult)

        hid_planes = [sb("hid_planes%d" % j, [P, PLANES, PEOPLE], BF16) for j in range(2)]
        for t in range(PLANES):
            for j in range(2):
                looked_up = group[t][:].indirect(entries(per_t, PEOPLE * j, PEOPLE))
                if t >= FIRST_SHARED_PLANE and j == 0:
                    nc.vector.tensor_copy(hid_planes[j][:, t, :], looked_up)
                else:
                    nc.scalar.activation(hid_planes[j][:, t, :], looked_up, ACT.Copy)

        hid = [sb("hid%d" % j, [P, PEOPLE, PLANES], BF16) for j in range(2)]
        hid_words = [sb("hid_words%d" % j, [P, PEOPLE], U32) for j in range(2)]
        hid_scales = [sb("hid_scales%d" % j, [P, PEOPLE], U8) for j in range(2)]

        def interleave(copy, j, people):
            copy(
                hid[j][:, people, :].rearrange("p (c i) t -> p c t i", i=4),
                hid_planes[j][:, :, people].rearrange("p t (c i) -> p c t i", i=4),
            )

        interleave(nc.vector.tensor_copy, 0, slice(0, PEOPLE))
        interleave(nc.vector.tensor_copy, 1, slice(0, PEOPLE // 2))
        interleave(nc.scalar.copy, 1, slice(PEOPLE // 2, PEOPLE))
        for j in range(2):
            nc.vector.quantize_mx(
                out=hid_words[j][:].bitcast(FP8X4), scales=hid_scales[j][:], in_=hid[j][:].rearrange("p r t -> p (r t)")
            )
        for j, queue in enumerate((nc.sync, nc.scalar)):
            acc = bank(HALVES * LAST + j, PEOPLE)
            nc.tensor.matmul_mx(
                out=acc[:],
                lhsT=w3w.bitcast(FP4X4),
                lhsT_scale=w3s,
                rhs=hid_words[j][:].bitcast(FP8X4),
                rhs_scale=hid_scales[j][:],
                start=True,
                stop=True,
            )
            result = sb("result%d" % j, [P, PEOPLE], F32)
            nc.scalar.copy(result[:], acc[:])
            queue.dma_start(out=out[:, PEOPLE * j : PEOPLE * (j + 1)], in_=result[:])
